import numpy as np
import ml_dtypes


def mxq(x, axis, fmt="e4m3"):
    dtype, down = {"e4m3": (ml_dtypes.float8_e4m3fn, 7), "e5m2": (ml_dtypes.float8_e5m2, 14)}[fmt]
    v = np.moveaxis(np.asarray(x, np.float32).astype(ml_dtypes.bfloat16).astype(np.float64), axis, -1)
    blocks = v.reshape(v.shape[:-1] + (-1, 32))
    amax = np.abs(blocks).max(-1, keepdims=True)
    byte = np.maximum(np.where(amax > 0, np.frexp(amax)[1] - 1 + 127, 0) - down, 1)
    scale = np.exp2(byte - 127.0)
    codes = (blocks / scale).astype(np.float32).astype(dtype).astype(np.float64)
    return np.moveaxis((codes * scale).reshape(v.shape), -1, axis)


WIDE = False


def mx_kscale(k):
    if not WIDE:
        return np.ones(k)
    levels = np.array([10, -10, 5, -5, 0])
    if k % 512:
        return np.exp2(np.random.permutation(np.resize(levels, k // 32))).repeat(32)
    a = np.empty((k // 512, 16))
    for p in range(k // 512):
        a[p, :8] = np.random.permutation(np.resize(levels, 8))
        for g in range(8):
            far = levels[np.abs(levels - a[p, g]) >= 10]
            a[p, g + 8] = far[np.random.randint(len(far))]
    return np.exp2(a.ravel()).repeat(32)


def f64(x):
    return np.asarray(x).astype(np.float64)


def striped(idx):
    return np.tile(idx.reshape(-1, 16).T, (8, 1)).astype(np.uint16)


def unstriped(offs):
    return offs[:16].T.reshape(-1).astype(np.int64)


def striped8(idx):
    return np.concatenate([x.reshape(-1, 16).T for x in idx]).astype(np.uint16)


def runs(offs, k):
    lists = np.stack([offs[16 * r : 16 * r + 16].T.reshape(-1) for r in range(8)]).astype(np.int64)
    return lists[np.arange(k) % 512 // 64]


def pack_weight(w):
    k, n = w.shape
    w = f64(np.asarray(w, np.float32).astype(ml_dtypes.bfloat16)).reshape(k // 32, 32, n)
    amax = np.abs(w).max(1)
    byte = np.clip(np.where(amax > 0, np.frexp(amax)[1] - 1 + 127 - 7, 1), 1, 254)
    scaled = (w * np.exp2(127.0 - byte)[:, None, :]).reshape(k, n).astype(np.float32)
    words = np.ascontiguousarray(scaled.reshape(k // 512, 128, 4, n).transpose(0, 1, 3, 2)).astype(ml_dtypes.float8_e4m3fn).view(np.uint8)
    return words, np.ascontiguousarray(byte.astype(np.uint8).reshape(k // 512, 16, n))


def unpack_weight(words, scales):
    g, p, n, _ = words.shape
    vals = np.ascontiguousarray(words).view(ml_dtypes.float8_e4m3fn).astype(np.float64) * np.repeat(np.exp2(scales.astype(np.float64) - 127.0), 8, axis=1)[..., None]
    return vals.transpose(0, 1, 3, 2).reshape(g * 512, n)


E2M1 = np.array([0.0, 0.5, 1.0, 1.5, 2.0, 3.0, 4.0, 6.0, -0.0, -0.5, -1.0, -1.5, -2.0, -3.0, -4.0, -6.0])


def pack_fp4(w):
    k, n = w.shape
    w = f64(np.asarray(w, np.float32).astype(ml_dtypes.bfloat16)).reshape(k // 32, 32, n)
    amax = np.abs(w).max(1)
    mant, ex = np.frexp(amax / 6.0)
    byte = np.clip(np.where(amax > 0, np.where(mant > 0.5, ex, ex - 1) + 127, 1), 1, 254)
    scaled = (w * np.exp2(127.0 - byte)[:, None, :]).reshape(k, n).astype(np.float32)
    c = np.ascontiguousarray(scaled.reshape(k // 512, 128, 4, n).transpose(0, 1, 3, 2)).astype(ml_dtypes.float4_e2m1fn).view(np.uint8) & 0xF
    words = (c[..., 0::2] | (c[..., 1::2] << 4)).reshape(k // 512, 128, 2 * n)
    return np.ascontiguousarray(words), np.ascontiguousarray(byte.astype(np.uint8).reshape(k // 512, 16, n))


def unpack_fp4(words, scales):
    g, _, n = scales.shape
    words = np.ascontiguousarray(words).reshape(g, 128, n, 2)
    nib = np.empty((g, 128, n, 4), np.uint8)
    nib[..., 0::2] = words & 0xF
    nib[..., 1::2] = words >> 4
    vals = E2M1[nib] * np.repeat(np.exp2(scales.astype(np.float64) - 127.0), 8, axis=1)[..., None]
    return vals.transpose(0, 1, 3, 2).reshape(g * 512, n)


def sigmoid(v):
    return 1.0 / (1.0 + np.exp(-np.maximum(v, -700.0)))

def planes(y):
    n, m = y.shape
    v = y.astype(np.float32).astype(ml_dtypes.bfloat16).astype(np.float64).reshape(n // 32, 32, m)
    top = np.abs(v).max(1)
    byte = np.clip(np.where(top > 0, np.frexp(top)[1] - 1 + 127 - 7, 1), 1, 254)
    codes = (v * np.exp2(127.0 - byte)[:, None, :]).reshape(n, m).astype(np.float32).astype(ml_dtypes.float8_e4m3fn).view(np.uint8)
    words = codes.reshape(n // 512, 128, 4, m).transpose(0, 1, 3, 2)
    return np.ascontiguousarray(words), np.ascontiguousarray(byte.astype(np.uint8).reshape(n // 512, 16, m))


K, T, S, N, H, W = 512, 2048, 512, 512, 512, 256


def setup_inputs():
    n = np.random.standard_normal
    s = mx_kscale(K)[:, None]
    u = mx_kscale(S)
    packed_xT = pack_weight(n((K, T)) * s)
    packed_w1 = pack_fp4(n((S, N)) / np.sqrt(S) / u[:, None])
    perm = np.stack([np.random.permutation(H) for _ in range(8)])
    return {
        "x_words": packed_xT[0],
        "x_scales": packed_xT[1],
        "wa": (n((K, H)) / np.sqrt(K) / s).astype(np.float32),
        "wb": (n((K, H)) / np.sqrt(K) / s).astype(np.float32),
        "gt": (np.random.uniform(0.5, 1.5, (S, 1)) * u[:, None]).astype(np.float32),
        "w1_words": packed_w1[0],
        "w1_scales": packed_w1[1],
        "offs": striped(np.random.permutation(T)[:S]),
        "two": striped(np.random.permutation(T)[:S]),
        "n1": striped8(np.stack([np.random.permutation(H) for _ in range(8)])),
        "n2": striped8(np.stack([np.random.permutation(H) for _ in range(8)])),
        "n3": striped8(perm[:, :W]),
        "n4": striped8(perm[:, W:]),
    }


def reference(x_words, x_scales, wa, wb, gt, w1_words, w1_scales, offs, two, n1, n2, n3, n4):
    xq = unpack_weight(x_words, x_scales)[:, unstriped(offs)]
    y = xq.T @ mxq(f64(wa), 0, "e4m3")
    x_two = unpack_weight(x_words, x_scales)[:, unstriped(two)]
    d = x_two.T @ mxq(f64(wb), 0, "e4m3")
    z = f64(gt) * ((y - (y[np.arange(S)[:, None], runs(n1, S)])) / (np.abs(d) + np.abs(d[np.arange(S)[:, None], runs(n2, S)]) + 0.5))
    h = unpack_fp4(w1_words, w1_scales).T @ mxq(z, 0, "e4m3")
    pb = h[np.arange(N)[:, None], runs(n4, N)]
    pa = h[np.arange(N)[:, None], runs(n3, N)]
    rb = pb * sigmoid(pb - pa)
    ra = pa * sigmoid(pa - pb)
    ds = np.zeros((N, H))
    ds[np.arange(N)[:, None], runs(n3, N)] = ra
    out = ds.copy()
    out[np.arange(N)[:, None], runs(n4, N)] = rb
    return (out,) + planes(out)

@@ -1,0 +1,282 @@
+from contextlib import ExitStack
+
+import concourse.mybir as mybir
+
+K, T, S, N, H, W = 512, 2048, 512, 512, 512, 256
+FLOPS = 2 * K * S * H * 2 + 2 * S * N * H
+
+F32 = mybir.dt.float32
+BF16 = mybir.dt.bfloat16
+I32 = mybir.dt.int32
+U32 = mybir.dt.uint32
+U16 = mybir.dt.uint16
+U8 = mybir.dt.uint8
+FP8X4 = mybir.dt.float8_e4m3fn_x4
+FP4X4 = mybir.dt.float4_e2m1fn_x4
+ALU = mybir.AluOpType
+ACT = mybir.ActivationFunctionType
+
+P = 128
+PACK = 4
+HALF = H // 2
+QUADS = 4
+
+
+def tile_picked_twtnormbduel_none_po_kernel(
+    tc, x_words, x_scales, wa, wb, gt, w1_words, w1_scales, offs, two, n1, n2, n3, n4, out_0, out_1, out_2
+):
+    nc = tc.nc
+    halves = [slice(0, HALF), slice(HALF, H)]
+
+    with ExitStack() as ctx:
+        keep = ctx.enter_context(tc.tile_pool(name="keep", bufs=1))
+        psum = ctx.enter_context(tc.psum_pool(name="psum", bufs=1))
+
+        def sb(name, shape, dtype, tag=None):
+            return keep.tile(shape, dtype, name=name, tag=tag or name, align_bytes=64)
+
+        def load_list(name, src):
+            tile = keep.tile(list(src.shape), U16, name=name)
+            nc.sync.dma_start(tile[:], src)
+            return tile
+
+        def load_scale_rows(queue, tile, src):
+            for q in range(QUADS):
+                queue.dma_start(out=tile[32 * q : 32 * q + 4, :].bitcast(I32), in_=src[0, 4 * q : 4 * q + 4, :].bitcast(I32))
+
+        x_scale_table = sb("x_scale_table", [P, T], U8)
+        nc.vector.memset(x_scale_table[:].bitcast(I32), 0)
+        w1_scale_raw = sb("w1_scale_raw", [P, N], U8)
+        nc.vector.memset(w1_scale_raw[:].bitcast(I32), 0)
+        half_const = sb("half_const", [P, 1], F32)
+        nc.vector.memset(half_const[:], 0.5)
+        warm = sb("warm", [P, 1], F32)
+        nc.scalar.activation(warm[:], half_const[:], ACT.Abs_reciprocal_sqrt)
+
+        two_list = load_list("two_list", two)
+        offs_list = load_list("offs_list", offs)
+        load_scale_rows(nc.sync, x_scale_table, x_scales)
+        x_word_table = sb("x_word_table", [P, T], I32)
+        nc.sync.dma_start(out=x_word_table[:], in_=x_words[0].rearrange("p n t -> p (n t)").bitcast(I32))
+
+        def load_weight(name, src):
+            rows = src.rearrange("(p j) w -> p j w", j=PACK)
+            raws = []
+            for u, cols in enumerate(halves):
+                raw = sb("%s_raw%d" % (name, u), [P, PACK, HALF], F32)
+                nc.sync.dma_start(out=raw[:], in_=rows[:, :, cols])
+                raws.append(raw)
+            return raws
+
+        wb_raw = load_weight("wb", wb)
+        n2_list = load_list("n2_list", n2)
+        wa_raw = load_weight("wa", wa)
+        gt_sb = sb("gt_sb", [P, PACK], F32)
+        nc.sync.dma_start(out=gt_sb[:], in_=gt.rearrange("(p t) o -> p (t o)", t=PACK))
+        n1_list = load_list("n1_list", n1)
+        w1_word_raw = sb("w1_word_raw", [P, 2 * N], U8)
+        nc.sync.dma_start(out=w1_word_raw[:].bitcast(I32), in_=w1_words[0].bitcast(I32))
+        load_scale_rows(nc.sync, w1_scale_raw, w1_scales)
+        n3_list = load_list("n3_list", n3)
+        n4_list = load_list("n4_list", n4)
+
+        def pick_scales(name, offsets):
+            picked = sb(name + "_picked_scales", [P, S], U8)
+            nc.vector.tensor_copy(picked[:], x_scale_table[:].indirect(offsets[:]))
+            return picked
+
+        def deal_bytes(name, src, tag=None):
+            dealt = sb(name + "_dealt_scales", [P, S], U8, tag)
+            nc.vector.tensor_copy(
+                out=dealt[:].rearrange("p (t m) -> p t m", t=PACK), in_=src[:].rearrange("p (m t) -> p t m", t=PACK)
+            )
+            return dealt
+
+        def pick_words(name, offsets, tag=None):
+            picked = sb(name + "_picked_words", [P, S], U32, tag)
+            nc.vector.tensor_copy(picked[:], x_word_table[:].bitcast(U32).indirect(offsets[:]))
+            return picked
+
+        def deal_words(name, src):
+            dealt = sb(name + "_dealt_words", [P, S], I32)
+            nc.vector.tensor_copy(
+                out=dealt[:].rearrange("p (t c i) -> p c t i", t=PACK, i=4),
+                in_=src[:].bitcast(I32).rearrange("p (c i t) -> p c t i", t=PACK, i=4),
+            )
+            return dealt
+
+        def round_weight(name, raw):
+            grouped = sb(name, [P, HALF * PACK], BF16)
+            nc.scalar.copy(
+                out=grouped[:].rearrange("p (c i t) -> p c t i", t=PACK, i=4),
+                in_=raw[:].rearrange("p t (c i) -> p c t i", i=4),
+            )
+            return grouped
+
+        def quantize(codes, scales, cols, grouped):
+            nc.vector.quantize_mx(out=codes[:, cols].bitcast(FP8X4), scales=scales[:, cols], in_=grouped)
+
+        two_picked_scales = pick_scales("two", two_list)
+        offs_picked_scales = pick_scales("offs", offs_list)
+        two_scales = deal_bytes("two", two_picked_scales)
+        two_picked_words = pick_words("two", two_list)
+        offs_scales = deal_bytes("offs", offs_picked_scales)
+        two_words = deal_words("two", two_picked_words)
+
+        def quantize_weight_half(name, raws, codes, scales, u):
+            grouped = round_weight("%s_grouped%d" % (name, u), raws[u])
+            quantize(codes, scales, halves[u], grouped[:])
+
+        def project(first_bank, words, scales, w_codes, w_scales):
+            banks = []
+            for t in range(PACK):
+                bank = psum.tile([P, H], F32, name="proj%d" % (first_bank + t), tag="bank%d" % (first_bank + t))
+                rows = slice(t * P, (t + 1) * P)
+                nc.tensor.matmul_mx(
+                    out=bank[:],
+                    lhsT=words[:, rows].bitcast(FP8X4),
+                    lhsT_scale=scales[:, rows],
+                    rhs=w_codes[:].bitcast(FP8X4),
+                    rhs_scale=w_scales[:],
+                    start=True,
+                    stop=True,
+                )
+                banks.append(bank)
+            return banks
+
+        wb_codes, wb_scales = sb("wb_codes", [P, H], U32), sb("wb_scales", [P, H], U8)
+        wa_codes, wa_scales = sb("wa_codes", [P, H], U32), sb("wa_scales", [P, H], U8)
+        quantize_weight_half("wb", wb_raw, wb_codes, wb_scales, 0)
+        quantize_weight_half("wb", wb_raw, wb_codes, wb_scales, 1)
+        d_banks = project(0, two_words, two_scales, wb_codes, wb_scales)
+        offs_picked_words = pick_words("offs", offs_list, "wb_grouped1")
+        offs_words = deal_words("offs", offs_picked_words)
+        quantize_weight_half("wa", wa_raw, wa_codes, wa_scales, 0)
+
+        neg_gt = sb("neg_gt", [P, PACK], F32)
+        nc.gpsimd.tensor_scalar(out=neg_gt[:], in0=gt_sb[:], scalar1=-1.0, scalar2=0.0, op0=ALU.mult, op1=ALU.add)
+
+        steps = 2 * PACK
+        windows = [sb("window0", [P, H], F32)] + [sb("window%d" % k, [P, 2 * H], F32) for k in range(1, steps)]
+        last_plain = sb("last_plain", [P, H], F32)
+        plains = [windows[k + 1][:, H:] for k in range(steps - 1)] + [last_plain[:]]
+        DUP = "VVVDDDDD"
+
+        def leave_psum(k):
+            own = windows[k][:, :H]
+            if k < PACK:
+                nc.scalar.activation(own, d_banks[k][:], ACT.Abs)
+            else:
+                nc.scalar.activation(own, y_banks[k - PACK][:], ACT.Copy, scale=neg_gt[:, k - PACK : k - PACK + 1])
+            if DUP[k] == "S":
+                if k < PACK:
+                    nc.scalar.activation(plains[k], d_banks[k][:], ACT.Abs)
+                else:
+                    nc.scalar.activation(plains[k], y_banks[k - PACK][:], ACT.Copy, scale=neg_gt[:, k - PACK : k - PACK + 1])
+            elif DUP[k] == "V":
+                nc.vector.tensor_copy(out=plains[k], in_=own)
+            else:
+                nc.sync.dma_start(out=plains[k], in_=own)
+
+        den = sb("den", [P, PACK, H], F32)
+        num = sb("num", [P, PACK, H], F32)
+        root = sb("root", [P, PACK, H], F32)
+        recip = sb("recip", [P, PACK, H], F32)
+        leave_psum(0)
+        quantize_weight_half("wa", wa_raw, wa_codes, wa_scales, 1)
+        y_banks = project(PACK, offs_words, offs_scales, wa_codes, wa_scales)
+        for k in range(1, steps):
+            leave_psum(k)
+        for t in range(PACK):
+            if t == 0:
+                for u, cols in enumerate(halves):
+                    nc.vector.tensor_tensor(
+                        den[:, 0, cols], windows[0][:].indirect(n2_list[:, 16 * u : 16 * u + 16]), plains[0][:, cols], ALU.add
+                    )
+            else:
+                nc.vector.tensor_tensor(den[:, t, :], windows[t][:].indirect(n2_list[:]), plains[t], ALU.add)
+        for t in range(PACK):
+            nc.scalar.activation(root[:, t, :], den[:, t, :], ACT.Abs_reciprocal_sqrt, bias=half_const[:])
+            nc.scalar.activation(recip[:, t, :], root[:, t, :], ACT.Square)
+        for t in range(PACK):
+            nc.vector.tensor_tensor(num[:, t, :], windows[PACK + t][:].indirect(n1_list[:]), plains[PACK + t], ALU.subtract)
+
+        w1_dealt_words = sb("w1_dealt_words", [P, 2 * N], U8, "wa_grouped1")
+        nc.vector.tensor_copy(
+            out=w1_dealt_words[:].rearrange("p (t m b) -> p t m b", t=PACK, b=2),
+            in_=w1_word_raw[:].rearrange("p (m t b) -> p t m b", t=PACK, b=2),
+        )
+        w1_dealt_scales = deal_bytes("w1", w1_scale_raw, "wa_raw1")
+
+        z_codes = sb("z_codes", [P, H], U32)
+        z_scales = sb("z_scales", [P, H], U8)
+        z_grouped = []
+        for u, cols in enumerate(halves):
+            grouped = sb("z_grouped%d" % u, [P, HALF * PACK], BF16)
+            nc.vector.tensor_tensor(
+                grouped[:].rearrange("p (c i t) -> p c t i", t=PACK, i=4),
+                num[:, :, cols].rearrange("p t (c i) -> p c t i", i=4),
+                recip[:, :, cols].rearrange("p t (c i) -> p c t i", i=4),
+                ALU.mult,
+            )
+            z_grouped.append(grouped)
+        for u, cols in enumerate(halves):
+            quantize(z_codes, z_scales, cols, z_grouped[u][:])
+
+        order = [2, 0, 1, 3]
+        h_rows = {t: sb("h_rows%d" % t, [P, H], F32) for t in order}
+        for u, cols in enumerate(halves):
+            for t in order:
+                bank = psum.tile([P, H], F32, name="mix%d_%d" % (t, u), tag="bank%d" % (PACK * u + t))
+                nc.tensor.matmul_mx(
+                    out=bank[:, :HALF],
+                    lhsT=w1_dealt_words[:, 2 * P * t : 2 * P * (t + 1)].bitcast(FP4X4),
+                    lhsT_scale=w1_dealt_scales[:, P * t : P * (t + 1)],
+                    rhs=z_codes[:, cols].bitcast(FP8X4),
+                    rhs_scale=z_scales[:, cols],
+                    start=True,
+                    stop=True,
+                )
+                nc.scalar.copy(out=h_rows[t][:, cols], in_=bank[:, :HALF])
+
+        out_rows = out_0.rearrange("(p t) n -> p t n", t=PACK)
+        out_grouped = sb("out_grouped", [P, H, PACK], BF16)
+        pairs, gates, results = {}, {}, {}
+
+        def fetch(t):
+            pair = sb("pair%d" % t, [P, 2, W], F32)
+            nc.vector.tensor_copy(pair[:, 0, :], h_rows[t][:].indirect(n3_list[:]))
+            nc.vector.tensor_copy(pair[:, 1, :], h_rows[t][:].indirect(n4_list[:]))
+            diff = sb("diff%d" % t, [P, W], F32)
+            nc.vector.tensor_tensor(diff[:], pair[:, 1, :], pair[:, 0, :], ALU.subtract)
+            gate = sb("gate%d" % t, [P, 2, W], F32)
+            nc.scalar.activation(gate[:, 0, :], diff[:], ACT.Sigmoid, scale=-1.0)
+            nc.scalar.activation(gate[:, 1, :], diff[:], ACT.Sigmoid)
+            pairs[t], gates[t] = pair, gate
+
+        def put(t):
+            result = sb("result%d" % t, [P, H], F32)
+            nc.vector.tensor_tensor(result[:].indirect(n3_list[:]), pairs[t][:, 0, :], gates[t][:, 0, :], ALU.mult)
+            nc.vector.tensor_tensor(result[:].indirect(n4_list[:]), pairs[t][:, 1, :], gates[t][:, 1, :], ALU.mult)
+            nc.sync.dma_start(out=out_rows[:, t, :], in_=result[:])
+            results[t] = result
+            if t != order[-1]:
+                nc.scalar.copy(out=out_grouped[:, :, t], in_=result[:])
+
+        fetch(order[0])
+        for a in range(1, PACK):
+            fetch(order[a])
+            put(order[a - 1])
+        put(order[-1])
+
+        out_codes = sb("out_codes", [P, H], U32)
+        out_scales = sb("out_scales", [P, H], U8)
+        for cols in halves:
+            nc.vector.tensor_copy(out=out_grouped[:, cols, order[-1]], in_=results[order[-1]][:, cols])
+        out_words = out_1[0].rearrange("p n t -> p (n t)").bitcast(I32)
+        for cols in halves:
+            quantize(out_codes, out_scales, cols, out_grouped[:, cols, :].rearrange("p n t -> p (n t)"))
+            nc.sync.dma_start(out=out_words[:, cols], in_=out_codes[:, cols].bitcast(I32))
+        for q in range(QUADS):
+            queue = nc.scalar if q % 2 else nc.sync
+            queue.dma_start(out=out_2[0, 4 * q : 4 * q + 4, :].bitcast(I32), in_=out_scales[32 * q : 32 * q + 4, :].bitcast(I32))

@@ -1,6 +1,7 @@
 from contextlib import ExitStack
 
 import concourse.mybir as mybir
+from concourse.masks import make_identity
 
 K, T, S, N, H, W = 512, 2048, 512, 512, 512, 256
 FLOPS = 2 * K * S * H * 2 + 2 * S * N * H
@@ -35,14 +36,17 @@ def tile_picked_twtnormbduel_none_po_kernel(
         def sb(name, shape, dtype, tag=None):
             return keep.tile(shape, dtype, name=name, tag=tag or name, align_bytes=64)
 
+        def bank(name, number):
+            return psum.tile([P, H], F32, name=name, tag="bank%d" % number)
+
         def load_list(name, src):
             tile = keep.tile(list(src.shape), U16, name=name)
             nc.sync.dma_start(tile[:], src)
             return tile
 
-        def load_scale_rows(queue, tile, src):
+        def load_scale_rows(tile, src):
             for q in range(QUADS):
-                queue.dma_start(out=tile[32 * q : 32 * q + 4, :].bitcast(I32), in_=src[0, 4 * q : 4 * q + 4, :].bitcast(I32))
+                nc.sync.dma_start(out=tile[32 * q : 32 * q + 4, :].bitcast(I32), in_=src[0, 4 * q : 4 * q + 4, :].bitcast(I32))
 
         x_scale_table = sb("x_scale_table", [P, T], U8)
         nc.vector.memset(x_scale_table[:].bitcast(I32), 0)
@@ -52,10 +56,12 @@ def tile_picked_twtnormbduel_none_po_kernel(
         nc.vector.memset(half_const[:], 0.5)
         warm = sb("warm", [P, 1], F32)
         nc.scalar.activation(warm[:], half_const[:], ACT.Abs_reciprocal_sqrt)
+        identity = sb("identity", [P, P], F32)
+        make_identity(nc, identity[:])
 
         two_list = load_list("two_list", two)
         offs_list = load_list("offs_list", offs)
-        load_scale_rows(nc.sync, x_scale_table, x_scales)
+        load_scale_rows(x_scale_table, x_scales)
         x_word_table = sb("x_word_table", [P, T], I32)
         nc.sync.dma_start(out=x_word_table[:], in_=x_words[0].rearrange("p n t -> p (n t)").bitcast(I32))
 
@@ -69,28 +75,16 @@ def tile_picked_twtnormbduel_none_po_kernel(
             return raws
 
         wb_raw = load_weight("wb", wb)
-        n2_list = load_list("n2_list", n2)
         wa_raw = load_weight("wa", wa)
+        n2_list = load_list("n2_list", n2)
         gt_sb = sb("gt_sb", [P, PACK], F32)
         nc.sync.dma_start(out=gt_sb[:], in_=gt.rearrange("(p t) o -> p (t o)", t=PACK))
-        n1_list = load_list("n1_list", n1)
         w1_word_raw = sb("w1_word_raw", [P, 2 * N], U8)
         nc.sync.dma_start(out=w1_word_raw[:].bitcast(I32), in_=w1_words[0].bitcast(I32))
-        load_scale_rows(nc.sync, w1_scale_raw, w1_scales)
+        load_scale_rows(w1_scale_raw, w1_scales)
+        n1_list = load_list("n1_list", n1)
         n3_list = load_list("n3_list", n3)
         n4_list = load_list("n4_list", n4)
-
-        def pick_scales(name, offsets):
-            picked = sb(name + "_picked_scales", [P, S], U8)
-            nc.vector.tensor_copy(picked[:], x_scale_table[:].indirect(offsets[:]))
-            return picked
-
-        def deal_bytes(name, src, tag=None):
-            dealt = sb(name + "_dealt_scales", [P, S], U8, tag)
-            nc.vector.tensor_copy(
-                out=dealt[:].rearrange("p (t m) -> p t m", t=PACK), in_=src[:].rearrange("p (m t) -> p t m", t=PACK)
-            )
-            return dealt
 
         def pick_words(name, offsets, tag=None):
             picked = sb(name + "_picked_words", [P, S], U32, tag)
@@ -105,35 +99,24 @@ def tile_picked_twtnormbduel_none_po_kernel(
             )
             return dealt
 
-        def round_weight(name, raw):
-            grouped = sb(name, [P, HALF * PACK], BF16)
-            nc.scalar.copy(
-                out=grouped[:].rearrange("p (c i t) -> p c t i", t=PACK, i=4),
-                in_=raw[:].rearrange("p t (c i) -> p c t i", i=4),
-            )
-            return grouped
-
         def quantize(codes, scales, cols, grouped):
             nc.vector.quantize_mx(out=codes[:, cols].bitcast(FP8X4), scales=scales[:, cols], in_=grouped)
 
-        two_picked_scales = pick_scales("two", two_list)
-        offs_picked_scales = pick_scales("offs", offs_list)
-        two_scales = deal_bytes("two", two_picked_scales)
-        two_picked_words = pick_words("two", two_list)
-        offs_scales = deal_bytes("offs", offs_picked_scales)
-        two_words = deal_words("two", two_picked_words)
-
         def quantize_weight_half(name, raws, codes, scales, u):
-            grouped = round_weight("%s_grouped%d" % (name, u), raws[u])
+            grouped = sb("%s_grouped%d" % (name, u), [P, HALF * PACK], BF16)
+            nc.scalar.copy(
+                out=grouped[:].rearrange("p (c i t) -> p c t i", t=PACK, i=4),
+                in_=raws[u][:].rearrange("p t (c i) -> p c t i", i=4),
+            )
             quantize(codes, scales, halves[u], grouped[:])
 
         def project(first_bank, words, scales, w_codes, w_scales):
             banks = []
             for t in range(PACK):
-                bank = psum.tile([P, H], F32, name="proj%d" % (first_bank + t), tag="bank%d" % (first_bank + t))
+                acc = bank("proj%d" % (first_bank + t), first_bank + t)
                 rows = slice(t * P, (t + 1) * P)
                 nc.tensor.matmul_mx(
-                    out=bank[:],
+                    out=acc[:],
                     lhsT=words[:, rows].bitcast(FP8X4),
                     lhsT_scale=scales[:, rows],
                     rhs=w_codes[:].bitcast(FP8X4),
@@ -141,72 +124,102 @@ def tile_picked_twtnormbduel_none_po_kernel(
                     start=True,
                     stop=True,
                 )
-                banks.append(bank)
+                banks.append(acc)
             return banks
+
+        picked_scales = sb("picked_scales", [P, 2, S], U8)
+        nc.vector.tensor_copy(picked_scales[:, 0, :], x_scale_table[:].indirect(two_list[:]))
+        nc.vector.tensor_copy(picked_scales[:, 1, :], x_scale_table[:].indirect(offs_list[:]))
+        two_picked_words = pick_words("two", two_list)
+        dealt_scales = sb("dealt_scales", [P, 2, S], U8)
+        nc.vector.tensor_copy(
+            out=dealt_scales[:].rearrange("p l (t m) -> p l t m", t=PACK),
+            in_=picked_scales[:].rearrange("p l (m t) -> p l t m", t=PACK),
+        )
+        two_words = deal_words("two", two_picked_words)
 
         wb_codes, wb_scales = sb("wb_codes", [P, H], U32), sb("wb_scales", [P, H], U8)
         wa_codes, wa_scales = sb("wa_codes", [P, H], U32), sb("wa_scales", [P, H], U8)
         quantize_weight_half("wb", wb_raw, wb_codes, wb_scales, 0)
         quantize_weight_half("wb", wb_raw, wb_codes, wb_scales, 1)
-        d_banks = project(0, two_words, two_scales, wb_codes, wb_scales)
+        d_banks = project(0, two_words, dealt_scales[:, 0, :], wb_codes, wb_scales)
         offs_picked_words = pick_words("offs", offs_list, "wb_grouped1")
-        offs_words = deal_words("offs", offs_picked_words)
         quantize_weight_half("wa", wa_raw, wa_codes, wa_scales, 0)
-
-        neg_gt = sb("neg_gt", [P, PACK], F32)
-        nc.gpsimd.tensor_scalar(out=neg_gt[:], in0=gt_sb[:], scalar1=-1.0, scalar2=0.0, op0=ALU.mult, op1=ALU.add)
+        offs_words = deal_words("offs", offs_picked_words)
 
         steps = 2 * PACK
-        windows = [sb("window0", [P, H], F32)] + [sb("window%d" % k, [P, 2 * H], F32) for k in range(1, steps)]
-        last_plain = sb("last_plain", [P, H], F32)
-        plains = [windows[k + 1][:, H:] for k in range(steps - 1)] + [last_plain[:]]
-        DUP = "VVVDDDDD"
+        windows = [sb("window%d" % k, [P, H if k < 2 else 2 * H], F32) for k in range(steps)]
+        spare = sb("spare", [P, 2, H], F32)
+        mates = [windows[k + 2][:, H:] if k + 2 < steps else spare[:, k + 2 - steps, :] for k in range(steps)]
+        quarters = [slice(b * P, (b + 1) * P) for b in range(H // P)]
 
-        def leave_psum(k):
-            own = windows[k][:, :H]
-            if k < PACK:
-                nc.scalar.activation(own, d_banks[k][:], ACT.Abs)
-            else:
-                nc.scalar.activation(own, y_banks[k - PACK][:], ACT.Copy, scale=neg_gt[:, k - PACK : k - PACK + 1])
-            if DUP[k] == "S":
-                if k < PACK:
-                    nc.scalar.activation(plains[k], d_banks[k][:], ACT.Abs)
-                else:
-                    nc.scalar.activation(plains[k], y_banks[k - PACK][:], ACT.Copy, scale=neg_gt[:, k - PACK : k - PACK + 1])
-            elif DUP[k] == "V":
-                nc.vector.tensor_copy(out=plains[k], in_=own)
-            else:
-                nc.sync.dma_start(out=plains[k], in_=own)
+        def leave_d(t):
+            nc.scalar.activation(windows[t][:, :H], d_banks[t][:], ACT.Abs)
 
-        den = sb("den", [P, PACK, H], F32)
-        num = sb("num", [P, PACK, H], F32)
-        root = sb("root", [P, PACK, H], F32)
-        recip = sb("recip", [P, PACK, H], F32)
-        leave_psum(0)
-        quantize_weight_half("wa", wa_raw, wa_codes, wa_scales, 1)
-        y_banks = project(PACK, offs_words, offs_scales, wa_codes, wa_scales)
-        for k in range(1, steps):
-            leave_psum(k)
-        for t in range(PACK):
-            if t == 0:
+        def leave_y(t):
+            k = PACK + t
+            nc.scalar.activation(windows[k][:, :H], y_banks[t][:], ACT.Copy, scale=gt_sb[:, t : t + 1])
+            nc.sync.dma_start(out=mates[k], in_=windows[k][:, :H])
+
+        def fetch_d(t):
+            if t < 2:
                 for u, cols in enumerate(halves):
-                    nc.vector.tensor_tensor(
-                        den[:, 0, cols], windows[0][:].indirect(n2_list[:, 16 * u : 16 * u + 16]), plains[0][:, cols], ALU.add
-                    )
+                    nc.vector.tensor_copy(mates[t][:, cols], windows[t][:].indirect(n2_list[:, 16 * u : 16 * u + 16]))
             else:
-                nc.vector.tensor_tensor(den[:, t, :], windows[t][:].indirect(n2_list[:]), plains[t], ALU.add)
-        for t in range(PACK):
-            nc.scalar.activation(root[:, t, :], den[:, t, :], ACT.Abs_reciprocal_sqrt, bias=half_const[:])
-            nc.scalar.activation(recip[:, t, :], root[:, t, :], ACT.Square)
-        for t in range(PACK):
-            nc.vector.tensor_tensor(num[:, t, :], windows[PACK + t][:].indirect(n1_list[:]), plains[PACK + t], ALU.subtract)
+                nc.vector.tensor_copy(mates[t], windows[t][:].indirect(n2_list[:]))
 
-        w1_dealt_words = sb("w1_dealt_words", [P, 2 * N], U8, "wa_grouped1")
-        nc.vector.tensor_copy(
-            out=w1_dealt_words[:].rearrange("p (t m b) -> p t m b", t=PACK, b=2),
-            in_=w1_word_raw[:].rearrange("p (m t b) -> p t m b", t=PACK, b=2),
-        )
-        w1_dealt_scales = deal_bytes("w1", w1_scale_raw, "wa_raw1")
+        num = sb("num", [P, PACK, H], F32)
+        recip = sb("recip", [P, PACK, H], F32)
+
+        def invert(t):
+            den = bank("den%d" % t, t)
+            for b in quarters:
+                nc.tensor.matmul(den[:, b], lhsT=windows[t][:, b], rhs=identity[:], start=True, stop=False, is_transpose=True)
+                nc.tensor.matmul(den[:, b], lhsT=mates[t][:, b], rhs=identity[:], start=False, stop=True, is_transpose=True)
+            root = sb("root%d" % t, [P, H], F32)
+            nc.scalar.activation(root[:], den[:], ACT.Abs_reciprocal_sqrt, bias=half_const[:])
+            return root
+
+        def square(t, root):
+            back = bank("back%d" % t, t)
+            for b in quarters:
+                nc.tensor.transpose(back[:, b], root[:, b], identity[:])
+            nc.scalar.activation(recip[:, t, :], back[:], ACT.Square)
+
+        def deal_w1(parity, word_tag, scale_tag):
+            words = sb("w1_dealt_words%d" % parity, [P, 2, 2 * P], U8, word_tag)
+            nc.vector.tensor_copy(
+                out=words[:].rearrange("p s (m b) -> p s m b", b=2),
+                in_=w1_word_raw[:].rearrange("p (m s e b) -> p e s m b", s=2, e=2, b=2)[:, parity],
+            )
+            scales = sb("w1_dealt_scales%d" % parity, [P, 2, P], U8, scale_tag)
+            nc.vector.tensor_copy(
+                out=scales[:], in_=w1_scale_raw[:].rearrange("p (m s e) -> p e s m", s=2, e=2)[:, parity]
+            )
+            return words, scales
+
+        leave_d(0)
+        fetch_d(0)
+        quantize_weight_half("wa", wa_raw, wa_codes, wa_scales, 1)
+        y_banks = project(PACK, offs_words, dealt_scales[:, 1, :], wa_codes, wa_scales)
+        for t in range(1, PACK):
+            leave_d(t)
+        for t in range(PACK):
+            leave_y(t)
+        fetch_d(1)
+        fetch_d(2)
+        w1_dealt = [deal_w1(0, "wa_grouped1", "wa_raw1")]
+        fetch_d(3)
+        roots = [invert(t) for t in range(PACK)]
+        for t in range(PACK):
+            square(t, roots[t])
+        nc.scalar.activation(warm[:], recip[:, PACK - 1, 0:1], ACT.Sigmoid)
+        for t in range(PACK - 1):
+            nc.vector.tensor_tensor(num[:, t, :], windows[PACK + t][:].indirect(n1_list[:]), mates[PACK + t], ALU.subtract)
+        for u, cols in enumerate(halves):
+            nc.vector.tensor_tensor(
+                num[:, PACK - 1, cols], windows[-1][:].indirect(n1_list[:, 16 * u : 16 * u + 16]), mates[-1][:, cols], ALU.subtract
+            )
 
         z_codes = sb("z_codes", [P, H], U32)
         z_scales = sb("z_scales", [P, H], U8)
@@ -214,67 +227,100 @@ def tile_picked_twtnormbduel_none_po_kernel(
         for u, cols in enumerate(halves):
             grouped = sb("z_grouped%d" % u, [P, HALF * PACK], BF16)
             nc.vector.tensor_tensor(
-                grouped[:].rearrange("p (c i t) -> p c t i", t=PACK, i=4),
-                num[:, :, cols].rearrange("p t (c i) -> p c t i", i=4),
-                recip[:, :, cols].rearrange("p t (c i) -> p c t i", i=4),
+                grouped[:].rearrange("p (c i t) -> p c t i", t=PACK, i=2),
+                num[:, :, cols].rearrange("p t (c i) -> p c t i", i=2),
+                recip[:, :, cols].rearrange("p t (c i) -> p c t i", i=2),
                 ALU.mult,
             )
             z_grouped.append(grouped)
         for u, cols in enumerate(halves):
             quantize(z_codes, z_scales, cols, z_grouped[u][:])
+        w1_dealt.append(deal_w1(1, "z_grouped1", "z_grouped0"))
 
-        order = [2, 0, 1, 3]
+        order = [0, 2, 3, 1]
         h_rows = {t: sb("h_rows%d" % t, [P, H], F32) for t in order}
-        for u, cols in enumerate(halves):
-            for t in order:
-                bank = psum.tile([P, H], F32, name="mix%d_%d" % (t, u), tag="bank%d" % (PACK * u + t))
+
+        def mix(t):
+            words, scales = w1_dealt[t % 2]
+            for u, cols in enumerate(halves if t == order[0] else [slice(0, H)]):
+                acc = bank("mix%d_%d" % (t, u), PACK * u + t)
                 nc.tensor.matmul_mx(
-                    out=bank[:, :HALF],
-                    lhsT=w1_dealt_words[:, 2 * P * t : 2 * P * (t + 1)].bitcast(FP4X4),
-                    lhsT_scale=w1_dealt_scales[:, P * t : P * (t + 1)],
+                    out=acc[:, cols],
+                    lhsT=words[:, t // 2, :].bitcast(FP4X4),
+                    lhsT_scale=scales[:, t // 2, :],
                     rhs=z_codes[:, cols].bitcast(FP8X4),
                     rhs_scale=z_scales[:, cols],
                     start=True,
                     stop=True,
                 )
-                nc.scalar.copy(out=h_rows[t][:, cols], in_=bank[:, :HALF])
+                nc.scalar.activation(h_rows[t][:, cols], acc[:, cols], ACT.Copy, scale=-1.0)
 
         out_rows = out_0.rearrange("(p t) n -> p t n", t=PACK)
-        out_grouped = sb("out_grouped", [P, H, PACK], BF16)
         pairs, gates, results = {}, {}, {}
+        blocks = [slice(0, P), slice(P, W)]
 
-        def fetch(t):
+        diffs = {}
+
+        def fetch(t, neg_tag=None):
             pair = sb("pair%d" % t, [P, 2, W], F32)
             nc.vector.tensor_copy(pair[:, 0, :], h_rows[t][:].indirect(n3_list[:]))
             nc.vector.tensor_copy(pair[:, 1, :], h_rows[t][:].indirect(n4_list[:]))
-            diff = sb("diff%d" % t, [P, W], F32)
-            nc.vector.tensor_tensor(diff[:], pair[:, 1, :], pair[:, 0, :], ALU.subtract)
-            gate = sb("gate%d" % t, [P, 2, W], F32)
-            nc.scalar.activation(gate[:, 0, :], diff[:], ACT.Sigmoid, scale=-1.0)
-            nc.scalar.activation(gate[:, 1, :], diff[:], ACT.Sigmoid)
-            pairs[t], gates[t] = pair, gate
+            neg = sb("neg%d" % t, [P, W], F32, neg_tag)
+            nc.scalar.activation(neg[:], pair[:, 0, :], ACT.Copy, scale=-1.0)
+            turned = bank("turned%d" % t, t)
+            for b in blocks:
+                nc.tensor.matmul(turned[:, b], lhsT=neg[:, b], rhs=identity[:], start=True, stop=False, is_transpose=True)
+                nc.tensor.matmul(turned[:, b], lhsT=pair[:, 1, b], rhs=identity[:], start=False, stop=True, is_transpose=True)
+            staged = sb("staged%d" % t, [P, W], F32)
+            nc.scalar.copy(out=staged[:], in_=turned[:, :W])
+            diff = bank("diff%d" % t, PACK + t)
+            for b in blocks:
+                nc.tensor.transpose(diff[:, b], staged[:, b], identity[:])
+            pairs[t], diffs[t] = pair, diff
 
-        def put(t):
-            result = sb("result%d" % t, [P, H], F32)
-            nc.vector.tensor_tensor(result[:].indirect(n3_list[:]), pairs[t][:, 0, :], gates[t][:, 0, :], ALU.mult)
-            nc.vector.tensor_tensor(result[:].indirect(n4_list[:]), pairs[t][:, 1, :], gates[t][:, 1, :], ALU.mult)
-            nc.sync.dma_start(out=out_rows[:, t, :], in_=result[:])
-            results[t] = result
-            if t != order[-1]:
-                nc.scalar.copy(out=out_grouped[:, :, t], in_=result[:])
+        def gate(t, side, tag=None):
+            gates[t, side] = sb("gate%d_%d" % (t, side), [P, W], F32, tag)
+            nc.scalar.activation(gates[t, side][:], diffs[t][:, :W], ACT.Sigmoid, scale=(-1.0, 1.0)[side])
 
-        fetch(order[0])
-        for a in range(1, PACK):
-            fetch(order[a])
-            put(order[a - 1])
-        put(order[-1])
+        def put(t, side, tag=None):
+            if side == 0:
+                results[t] = sb("result%d" % t, [P, H], F32, tag)
+            offsets = (n3_list, n4_list)[side]
+            nc.vector.tensor_tensor(results[t][:].indirect(offsets[:]), pairs[t][:, side, :], gates[t, side][:], ALU.mult)
+            if side == 1:
+                nc.sync.dma_start(out=out_rows[:, t, :], in_=results[t][:])
+                if t != order[-1]:
+                    nc.scalar.copy(out=out_grouped[:, :, t], in_=results[t][:])
+
+        for t in order[:2]:
+            mix(t)
+        for a, t in enumerate(order):
+            fetch(t, "staged%d" % order[0] if a >= 2 else None)
+            gate(t, 0)
+            if a > 0:
+                gate(order[a - 1], 1, "staged%d" % t if a < PACK - 1 else None)
+            if a + 2 < PACK:
+                mix(order[a + 2])
+        gate(order[-1], 1)
+        out_grouped = sb("out_grouped", [P, H, PACK], BF16, "staged%d" % order[-1])
+        put(order[0], 0)
+        put(order[1], 0)
+        put(order[0], 1)
+        put(order[2], 0)
+        put(order[1], 1)
+        put(order[2], 1)
+        put(order[3], 0, "result%d" % order[0])
+        put(order[3], 1)
+
 
         out_codes = sb("out_codes", [P, H], U32)
         out_scales = sb("out_scales", [P, H], U8)
-        for cols in halves:
-            nc.vector.tensor_copy(out=out_grouped[:, cols, order[-1]], in_=results[order[-1]][:, cols])
+        last = order[-1]
+        nc.scalar.copy(out=out_grouped[:, quarters[0], last], in_=results[last][:, quarters[0]])
+        for cols in (halves[1], quarters[1]):
+            nc.vector.tensor_copy(out=out_grouped[:, cols, last], in_=results[last][:, cols])
         out_words = out_1[0].rearrange("p n t -> p (n t)").bitcast(I32)
-        for cols in halves:
+        for cols in reversed(halves):
             quantize(out_codes, out_scales, cols, out_grouped[:, cols, :].rearrange("p n t -> p (n t)"))
             nc.sync.dma_start(out=out_words[:, cols], in_=out_codes[:, cols].bitcast(I32))
         for q in range(QUADS):

from contextlib import ExitStack

import concourse.mybir as mybir
from concourse.masks import make_identity

K, T, S, N, H, W = 512, 2048, 512, 512, 512, 256
FLOPS = 2 * K * S * H * 2 + 2 * S * N * H

F32 = mybir.dt.float32
BF16 = mybir.dt.bfloat16
I32 = mybir.dt.int32
U32 = mybir.dt.uint32
U16 = mybir.dt.uint16
U8 = mybir.dt.uint8
FP8X4 = mybir.dt.float8_e4m3fn_x4
FP4X4 = mybir.dt.float4_e2m1fn_x4
ALU = mybir.AluOpType
ACT = mybir.ActivationFunctionType

P = 128
PACK = 4
HALF = H // 2
QUADS = 4


def tile_picked_twtnormbduel_none_po_kernel(
    tc, x_words, x_scales, wa, wb, gt, w1_words, w1_scales, offs, two, n1, n2, n3, n4, out_0, out_1, out_2
):
    nc = tc.nc
    halves = [slice(0, HALF), slice(HALF, H)]

    with ExitStack() as ctx:
        keep = ctx.enter_context(tc.tile_pool(name="keep", bufs=1))
        psum = ctx.enter_context(tc.psum_pool(name="psum", bufs=1))

        def sb(name, shape, dtype, tag=None):
            return keep.tile(shape, dtype, name=name, tag=tag or name, align_bytes=64)

        def bank(name, number):
            return psum.tile([P, H], F32, name=name, tag="bank%d" % number)

        def load_list(name, src):
            tile = keep.tile(list(src.shape), U16, name=name)
            nc.sync.dma_start(tile[:], src)
            return tile

        def load_scale_rows(tile, src):
            for q in range(QUADS):
                nc.sync.dma_start(out=tile[32 * q : 32 * q + 4, :].bitcast(I32), in_=src[0, 4 * q : 4 * q + 4, :].bitcast(I32))

        x_scale_table = sb("x_scale_table", [P, T], U8)
        nc.vector.memset(x_scale_table[:].bitcast(I32), 0)
        w1_scale_raw = sb("w1_scale_raw", [P, N], U8)
        nc.vector.memset(w1_scale_raw[:].bitcast(I32), 0)
        half_const = sb("half_const", [P, 1], F32)
        nc.vector.memset(half_const[:], 0.5)
        warm = sb("warm", [P, 1], F32)
        nc.scalar.activation(warm[:], half_const[:], ACT.Abs_reciprocal_sqrt)
        identity = sb("identity", [P, P], F32)
        make_identity(nc, identity[:])

        two_list = load_list("two_list", two)
        offs_list = load_list("offs_list", offs)
        load_scale_rows(x_scale_table, x_scales)
        x_word_table = sb("x_word_table", [P, T], I32)
        nc.sync.dma_start(out=x_word_table[:], in_=x_words[0].rearrange("p n t -> p (n t)").bitcast(I32))

        def load_weight(name, src):
            rows = src.rearrange("(p j) w -> p j w", j=PACK)
            raws = []
            for u, cols in enumerate(halves):
                raw = sb("%s_raw%d" % (name, u), [P, PACK, HALF], F32)
                nc.sync.dma_start(out=raw[:], in_=rows[:, :, cols])
                raws.append(raw)
            return raws

        wb_raw = load_weight("wb", wb)
        wa_raw = load_weight("wa", wa)
        n2_list = load_list("n2_list", n2)
        gt_sb = sb("gt_sb", [P, PACK], F32)
        nc.sync.dma_start(out=gt_sb[:], in_=gt.rearrange("(p t) o -> p (t o)", t=PACK))
        w1_word_raw = sb("w1_word_raw", [P, 2 * N], U8)
        nc.sync.dma_start(out=w1_word_raw[:].bitcast(I32), in_=w1_words[0].bitcast(I32))
        load_scale_rows(w1_scale_raw, w1_scales)
        n1_list = load_list("n1_list", n1)
        n3_list = load_list("n3_list", n3)
        n4_list = load_list("n4_list", n4)

        def pick_words(name, offsets, tag=None):
            picked = sb(name + "_picked_words", [P, S], U32, tag)
            nc.vector.tensor_copy(picked[:], x_word_table[:].bitcast(U32).indirect(offsets[:]))
            return picked

        def deal_words(name, src):
            dealt = sb(name + "_dealt_words", [P, S], I32)
            nc.vector.tensor_copy(
                out=dealt[:].rearrange("p (t c i) -> p c t i", t=PACK, i=4),
                in_=src[:].bitcast(I32).rearrange("p (c i t) -> p c t i", t=PACK, i=4),
            )
            return dealt

        def quantize(codes, scales, cols, grouped):
            nc.vector.quantize_mx(out=codes[:, cols].bitcast(FP8X4), scales=scales[:, cols], in_=grouped)

        def quantize_weight_half(name, raws, codes, scales, u):
            grouped = sb("%s_grouped%d" % (name, u), [P, HALF * PACK], BF16)
            nc.scalar.copy(
                out=grouped[:].rearrange("p (c i t) -> p c t i", t=PACK, i=4),
                in_=raws[u][:].rearrange("p t (c i) -> p c t i", i=4),
            )
            quantize(codes, scales, halves[u], grouped[:])

        def project(first_bank, words, scales, w_codes, w_scales):
            banks = []
            for t in range(PACK):
                acc = bank("proj%d" % (first_bank + t), first_bank + t)
                rows = slice(t * P, (t + 1) * P)
                nc.tensor.matmul_mx(
                    out=acc[:],
                    lhsT=words[:, rows].bitcast(FP8X4),
                    lhsT_scale=scales[:, rows],
                    rhs=w_codes[:].bitcast(FP8X4),
                    rhs_scale=w_scales[:],
                    start=True,
                    stop=True,
                )
                banks.append(acc)
            return banks

        picked_scales = sb("picked_scales", [P, 2, S], U8)
        nc.vector.tensor_copy(picked_scales[:, 0, :], x_scale_table[:].indirect(two_list[:]))
        nc.vector.tensor_copy(picked_scales[:, 1, :], x_scale_table[:].indirect(offs_list[:]))
        two_picked_words = pick_words("two", two_list)
        dealt_scales = sb("dealt_scales", [P, 2, S], U8)
        nc.vector.tensor_copy(
            out=dealt_scales[:].rearrange("p l (t m) -> p l t m", t=PACK),
            in_=picked_scales[:].rearrange("p l (m t) -> p l t m", t=PACK),
        )
        two_words = deal_words("two", two_picked_words)

        wb_codes, wb_scales = sb("wb_codes", [P, H], U32), sb("wb_scales", [P, H], U8)
        wa_codes, wa_scales = sb("wa_codes", [P, H], U32), sb("wa_scales", [P, H], U8)
        quantize_weight_half("wb", wb_raw, wb_codes, wb_scales, 0)
        quantize_weight_half("wb", wb_raw, wb_codes, wb_scales, 1)
        d_banks = project(0, two_words, dealt_scales[:, 0, :], wb_codes, wb_scales)
        offs_picked_words = pick_words("offs", offs_list, "wb_grouped1")
        quantize_weight_half("wa", wa_raw, wa_codes, wa_scales, 0)
        offs_words = deal_words("offs", offs_picked_words)

        steps = 2 * PACK
        windows = [sb("window%d" % k, [P, H if k < 2 else 2 * H], F32) for k in range(steps)]
        spare = sb("spare", [P, 2, H], F32)
        mates = [windows[k + 2][:, H:] if k + 2 < steps else spare[:, k + 2 - steps, :] for k in range(steps)]
        quarters = [slice(b * P, (b + 1) * P) for b in range(H // P)]

        def leave_d(t):
            nc.scalar.activation(windows[t][:, :H], d_banks[t][:], ACT.Abs)

        def leave_y(t):
            k = PACK + t
            nc.scalar.activation(windows[k][:, :H], y_banks[t][:], ACT.Copy, scale=gt_sb[:, t : t + 1])
            nc.sync.dma_start(out=mates[k], in_=windows[k][:, :H])

        def fetch_d(t):
            if t < 2:
                for u, cols in enumerate(halves):
                    nc.vector.tensor_copy(mates[t][:, cols], windows[t][:].indirect(n2_list[:, 16 * u : 16 * u + 16]))
            else:
                nc.vector.tensor_copy(mates[t], windows[t][:].indirect(n2_list[:]))

        num = sb("num", [P, PACK, H], F32)
        recip = sb("recip", [P, PACK, H], F32)

        def invert(t):
            den = bank("den%d" % t, t)
            for b in quarters:
                nc.tensor.matmul(den[:, b], lhsT=windows[t][:, b], rhs=identity[:], start=True, stop=False, is_transpose=True)
                nc.tensor.matmul(den[:, b], lhsT=mates[t][:, b], rhs=identity[:], start=False, stop=True, is_transpose=True)
            root = sb("root%d" % t, [P, H], F32)
            nc.scalar.activation(root[:], den[:], ACT.Abs_reciprocal_sqrt, bias=half_const[:])
            return root

        def square(t, root):
            back = bank("back%d" % t, t)
            for b in quarters:
                nc.tensor.transpose(back[:, b], root[:, b], identity[:])
            nc.scalar.activation(recip[:, t, :], back[:], ACT.Square)

        def deal_w1(parity, word_tag, scale_tag):
            words = sb("w1_dealt_words%d" % parity, [P, 2, 2 * P], U8, word_tag)
            nc.vector.tensor_copy(
                out=words[:].rearrange("p s (m b) -> p s m b", b=2),
                in_=w1_word_raw[:].rearrange("p (m s e b) -> p e s m b", s=2, e=2, b=2)[:, parity],
            )
            scales = sb("w1_dealt_scales%d" % parity, [P, 2, P], U8, scale_tag)
            nc.vector.tensor_copy(
                out=scales[:], in_=w1_scale_raw[:].rearrange("p (m s e) -> p e s m", s=2, e=2)[:, parity]
            )
            return words, scales

        leave_d(0)
        fetch_d(0)
        quantize_weight_half("wa", wa_raw, wa_codes, wa_scales, 1)
        y_banks = project(PACK, offs_words, dealt_scales[:, 1, :], wa_codes, wa_scales)
        for t in range(1, PACK):
            leave_d(t)
        for t in range(PACK):
            leave_y(t)
        fetch_d(1)
        fetch_d(2)
        w1_dealt = [deal_w1(0, "wa_grouped1", "wa_raw1")]
        fetch_d(3)
        roots = [invert(t) for t in range(PACK)]
        for t in range(PACK):
            square(t, roots[t])
        nc.scalar.activation(warm[:], recip[:, PACK - 1, 0:1], ACT.Sigmoid)
        for t in range(PACK - 1):
            nc.vector.tensor_tensor(num[:, t, :], windows[PACK + t][:].indirect(n1_list[:]), mates[PACK + t], ALU.subtract)
        for u, cols in enumerate(halves):
            nc.vector.tensor_tensor(
                num[:, PACK - 1, cols], windows[-1][:].indirect(n1_list[:, 16 * u : 16 * u + 16]), mates[-1][:, cols], ALU.subtract
            )

        z_codes = sb("z_codes", [P, H], U32)
        z_scales = sb("z_scales", [P, H], U8)
        z_grouped = []
        for u, cols in enumerate(halves):
            grouped = sb("z_grouped%d" % u, [P, HALF * PACK], BF16)
            nc.vector.tensor_tensor(
                grouped[:].rearrange("p (c i t) -> p c t i", t=PACK, i=2),
                num[:, :, cols].rearrange("p t (c i) -> p c t i", i=2),
                recip[:, :, cols].rearrange("p t (c i) -> p c t i", i=2),
                ALU.mult,
            )
            z_grouped.append(grouped)
        for u, cols in enumerate(halves):
            quantize(z_codes, z_scales, cols, z_grouped[u][:])
        w1_dealt.append(deal_w1(1, "z_grouped1", "z_grouped0"))

        order = [0, 2, 3, 1]
        h_rows = {t: sb("h_rows%d" % t, [P, H], F32) for t in order}

        def mix(t):
            words, scales = w1_dealt[t % 2]
            for u, cols in enumerate(halves if t == order[0] else [slice(0, H)]):
                acc = bank("mix%d_%d" % (t, u), PACK * u + t)
                nc.tensor.matmul_mx(
                    out=acc[:, cols],
                    lhsT=words[:, t // 2, :].bitcast(FP4X4),
                    lhsT_scale=scales[:, t // 2, :],
                    rhs=z_codes[:, cols].bitcast(FP8X4),
                    rhs_scale=z_scales[:, cols],
                    start=True,
                    stop=True,
                )
                nc.scalar.activation(h_rows[t][:, cols], acc[:, cols], ACT.Copy, scale=-1.0)

        out_rows = out_0.rearrange("(p t) n -> p t n", t=PACK)
        pairs, gates, results = {}, {}, {}
        blocks = [slice(0, P), slice(P, W)]

        diffs = {}

        def fetch(t, neg_tag=None):
            pair = sb("pair%d" % t, [P, 2, W], F32)
            nc.vector.tensor_copy(pair[:, 0, :], h_rows[t][:].indirect(n3_list[:]))
            nc.vector.tensor_copy(pair[:, 1, :], h_rows[t][:].indirect(n4_list[:]))
            neg = sb("neg%d" % t, [P, W], F32, neg_tag)
            nc.scalar.activation(neg[:], pair[:, 0, :], ACT.Copy, scale=-1.0)
            turned = bank("turned%d" % t, t)
            for b in blocks:
                nc.tensor.matmul(turned[:, b], lhsT=neg[:, b], rhs=identity[:], start=True, stop=False, is_transpose=True)
                nc.tensor.matmul(turned[:, b], lhsT=pair[:, 1, b], rhs=identity[:], start=False, stop=True, is_transpose=True)
            staged = sb("staged%d" % t, [P, W], F32)
            nc.scalar.copy(out=staged[:], in_=turned[:, :W])
            diff = bank("diff%d" % t, PACK + t)
            for b in blocks:
                nc.tensor.transpose(diff[:, b], staged[:, b], identity[:])
            pairs[t], diffs[t] = pair, diff

        def gate(t, side, tag=None):
            gates[t, side] = sb("gate%d_%d" % (t, side), [P, W], F32, tag)
            nc.scalar.activation(gates[t, side][:], diffs[t][:, :W], ACT.Sigmoid, scale=(-1.0, 1.0)[side])

        def put(t, side, tag=None):
            if side == 0:
                results[t] = sb("result%d" % t, [P, H], F32, tag)
            offsets = (n3_list, n4_list)[side]
            nc.vector.tensor_tensor(results[t][:].indirect(offsets[:]), pairs[t][:, side, :], gates[t, side][:], ALU.mult)
            if side == 1:
                nc.sync.dma_start(out=out_rows[:, t, :], in_=results[t][:])
                if t != order[-1]:
                    nc.scalar.copy(out=out_grouped[:, :, t], in_=results[t][:])

        for t in order[:2]:
            mix(t)
        for a, t in enumerate(order):
            fetch(t, "staged%d" % order[0] if a >= 2 else None)
            gate(t, 0)
            if a > 0:
                gate(order[a - 1], 1, "staged%d" % t if a < PACK - 1 else None)
            if a + 2 < PACK:
                mix(order[a + 2])
        gate(order[-1], 1)
        out_grouped = sb("out_grouped", [P, H, PACK], BF16, "staged%d" % order[-1])
        put(order[0], 0)
        put(order[1], 0)
        put(order[0], 1)
        put(order[2], 0)
        put(order[1], 1)
        put(order[2], 1)
        put(order[3], 0, "result%d" % order[0])
        put(order[3], 1)


        out_codes = sb("out_codes", [P, H], U32)
        out_scales = sb("out_scales", [P, H], U8)
        last = order[-1]
        nc.scalar.copy(out=out_grouped[:, quarters[0], last], in_=results[last][:, quarters[0]])
        for cols in (halves[1], quarters[1]):
            nc.vector.tensor_copy(out=out_grouped[:, cols, last], in_=results[last][:, cols])
        out_words = out_1[0].rearrange("p n t -> p (n t)").bitcast(I32)
        for cols in reversed(halves):
            quantize(out_codes, out_scales, cols, out_grouped[:, cols, :].rearrange("p n t -> p (n t)"))
            nc.sync.dma_start(out=out_words[:, cols], in_=out_codes[:, cols].bitcast(I32))
        for q in range(QUADS):
            queue = nc.scalar if q % 2 else nc.sync
            queue.dma_start(out=out_2[0, 4 * q : 4 * q + 4, :].bitcast(I32), in_=out_scales[32 * q : 32 * q + 4, :].bitcast(I32))
